import numpy as np
import ml_dtypes

BF16 = ml_dtypes.bfloat16


def bf(x):
    return np.asarray(x, np.float32).astype(BF16)


def f32(x):
    return np.asarray(x, np.float32)


def f64(x):
    return np.asarray(x).astype(np.float64)


def striped(idx):
    return np.concatenate([l.reshape(-1, 16).T for l in idx])


def rows(idx, k):
    return np.tile(np.repeat(idx, 16, axis=0), (k // (16 * 8), 1))


def look(tab, idx):
    return np.take_along_axis(f64(tab), rows(idx, len(tab)), axis=1)


K, S, V, N, M = 256, 2048, 2048, 2048, 256


def setup_inputs():
    return {"tab": f32(np.random.standard_normal((K, S))), "y": f32(np.random.standard_normal((K, V))), "w": bf(np.random.standard_normal((K, M)) / np.sqrt(K)), "offs": striped(np.stack([np.random.permutation(S)[:N] for _ in range(8)]))}


def reference(tab, y, w, offs):
    idx = np.stack([g.T.reshape(-1) for g in np.split(offs, 8)])
    t = look(tab, idx)
    x = np.maximum(t, 0.0) * f64(y)
    y = f64(w).T @ x
    return y

@@ -1,0 +1,49 @@
+import concourse.mybir as mybir
+
+P = 128
+PIECE = 512
+FLOPS = 2 * 256 * 256 * 2048
+
+F32, BF16, U16 = mybir.dt.float32, mybir.dt.bfloat16, mybir.dt.uint16
+RELU = mybir.ActivationFunctionType.Relu
+MULT = mybir.AluOpType.mult
+
+
+def tile_lookup_gate_relu_none_kernel(tc, tab, y, w, offs, out):
+    nc = tc.nc
+    rows, window_cols = tab.shape
+    out_rows, entries = out.shape
+    blocks, out_blocks, pieces = rows // P, out_rows // P, entries // PIECE
+    offset_cols = PIECE // 16
+
+    with (
+        tc.tile_pool(name="held", bufs=1) as held,
+        tc.psum_pool(name="psum", bufs=1) as psum,
+    ):
+        offsets = held.tile([P, entries // 16], U16, name="offsets")
+        nc.sync.dma_start(offsets[:], offs)
+        windows = [held.tile([P, window_cols], F32, name=f"window{b}") for b in range(blocks)]
+        for b in range(blocks):
+            nc.sync.dma_start(windows[b][:], tab[b * P : (b + 1) * P, :])
+        weights = held.tile([P, blocks, out_rows], BF16, name="weights")
+        nc.sync.dma_start(weights[:], w.rearrange("(b p) m -> p b m", p=P))
+
+        steps = [(b, i) for b in range(blocks) for i in range(pieces)]
+        stream = {}
+        for b, i in steps:
+            stream[b, i] = held.tile([P, PIECE], F32, name=f"stream{b}_{i}")
+            nc.sync.dma_start(stream[b, i][:], y[b * P : (b + 1) * P, i * PIECE : (i + 1) * PIECE])
+
+        banks = {(i, m): psum.tile([P, PIECE], F32, name=f"bank{i}_{m}") for i in range(pieces) for m in range(out_blocks)}
+        for b, i in steps:
+            gate = held.tile([P, PIECE], F32, name=f"gate{b}_{i}")
+            nc.scalar.activation(gate[:], windows[b][:].indirect(offsets[:, i * offset_cols : (i + 1) * offset_cols]), RELU)
+            x = held.tile([P, PIECE], BF16, name=f"x{b}_{i}")
+            nc.vector.tensor_tensor(x[:], gate[:], stream[b, i][:], MULT)
+            for m in range(out_blocks):
+                nc.tensor.matmul(banks[i, m][:], weights[:, b, m * P : (m + 1) * P], x[:], start=b == 0, stop=b == blocks - 1)
+            if b == blocks - 1:
+                for m in range(out_blocks):
+                    result = held.tile([P, PIECE], F32, name=f"result{i}_{m}")
+                    nc.vector.tensor_copy(result[:], banks[i, m][:])
+                    nc.sync.dma_start(out[m * P : (m + 1) * P, i * PIECE : (i + 1) * PIECE], result[:])

@@ -2,6 +2,9 @@ import concourse.mybir as mybir
 
 P = 128
 PIECE = 512
+HEAD = 2
+TAIL = 2
+BANKS = 8
 FLOPS = 2 * 256 * 256 * 2048
 
 F32, BF16, U16 = mybir.dt.float32, mybir.dt.bfloat16, mybir.dt.uint16
@@ -18,7 +21,7 @@ def tile_lookup_gate_relu_none_kernel(tc, tab, y, w, offs, out):
 
     with (
         tc.tile_pool(name="held", bufs=1) as held,
-        tc.psum_pool(name="psum", bufs=1) as psum,
+        tc.psum_pool(name="psum", bufs=BANKS) as psum,
     ):
         offsets = held.tile([P, entries // 16], U16, name="offsets")
         nc.sync.dma_start(offsets[:], offs)
@@ -26,24 +29,57 @@ def tile_lookup_gate_relu_none_kernel(tc, tab, y, w, offs, out):
         for b in range(blocks):
             nc.sync.dma_start(windows[b][:], tab[b * P : (b + 1) * P, :])
         weights = held.tile([P, blocks, out_rows], BF16, name="weights")
-        nc.sync.dma_start(weights[:], w.rearrange("(b p) m -> p b m", p=P))
 
-        steps = [(b, i) for b in range(blocks) for i in range(pieces)]
+        warm_in = held.tile([P, 8], F32, name="warm_in")
+        warm_out = held.tile([P, 8], F32, name="warm_out")
+        nc.vector.memset(warm_in[:], 0.0)
+        nc.scalar.activation(warm_out[:], warm_in[:], RELU)
+
+        steps = [(b, i) for b in range(blocks) for i in range(HEAD)]
+        steps += [(b, i) for i in range(HEAD, pieces) for b in range(blocks)]
         stream = {}
         for b, i in steps:
             stream[b, i] = held.tile([P, PIECE], F32, name=f"stream{b}_{i}")
             nc.sync.dma_start(stream[b, i][:], y[b * P : (b + 1) * P, i * PIECE : (i + 1) * PIECE])
+            if (b, i) == steps[0]:
+                nc.sync.dma_start(weights[:], w.rearrange("(b p) m -> p b m", p=P))
 
-        banks = {(i, m): psum.tile([P, PIECE], F32, name=f"bank{i}_{m}") for i in range(pieces) for m in range(out_blocks)}
-        for b, i in steps:
-            gate = held.tile([P, PIECE], F32, name=f"gate{b}_{i}")
-            nc.scalar.activation(gate[:], windows[b][:].indirect(offsets[:, i * offset_cols : (i + 1) * offset_cols]), RELU)
-            x = held.tile([P, PIECE], BF16, name=f"x{b}_{i}")
-            nc.vector.tensor_tensor(x[:], gate[:], stream[b, i][:], MULT)
+        gates = [held.tile([P, PIECE], F32, name=f"gate{k}") for k in range(blocks * HEAD)]
+        xs = [held.tile([P, PIECE], BF16, name=f"x{k}") for k in range(HEAD + 2)]
+        banks = {}
+
+        def parts(i):
+            width = PIECE // TAIL if i == pieces - 1 else PIECE
+            return [slice(first, first + width) for first in range(0, PIECE, width)]
+
+        def store(i, part):
             for m in range(out_blocks):
-                nc.tensor.matmul(banks[i, m][:], weights[:, b, m * P : (m + 1) * P], x[:], start=b == 0, stop=b == blocks - 1)
-            if b == blocks - 1:
-                for m in range(out_blocks):
-                    result = held.tile([P, PIECE], F32, name=f"result{i}_{m}")
-                    nc.vector.tensor_copy(result[:], banks[i, m][:])
-                    nc.sync.dma_start(out[m * P : (m + 1) * P, i * PIECE : (i + 1) * PIECE], result[:])
+                result = held.tile([P, part.stop - part.start], F32, name=f"result{i}_{part.start}_{m}")
+                if i >= pieces - 2 and m == 1:
+                    nc.scalar.copy(result[:], banks[i, part.start, m][:])
+                else:
+                    nc.vector.tensor_copy(result[:], banks[i, part.start, m][:])
+                nc.sync.dma_start(out[m * P : (m + 1) * P, i * PIECE + part.start : i * PIECE + part.stop], result[:])
+
+        x_of = {}
+        finished = []
+        for step, (b, i) in enumerate(steps):
+            gate = gates[step % len(gates)]
+            nc.scalar.activation(gate[:], windows[b][:].indirect(offsets[:, i * offset_cols : (i + 1) * offset_cols]), RELU)
+            x_of[b, i] = xs[step if step < HEAD else HEAD + step % 2]
+            multiplier = nc.gpsimd if step == blocks * HEAD else nc.vector
+            sum_order = (1, 0) if 0 < i < HEAD else (0, 1)
+            for part in parts(i):
+                multiplier.tensor_tensor(x_of[b, i][:, part], gate[:, part], stream[b, i][:, part], MULT)
+                for done in finished:
+                    store(*done)
+                finished = []
+                if b == blocks - 1:
+                    for m in range(out_blocks):
+                        bank = psum.tile([P, part.stop - part.start], F32, name="bank")
+                        for k in sum_order:
+                            nc.tensor.matmul(bank[:], weights[:, k, m * P : (m + 1) * P], x_of[k, i][:, part], start=k == sum_order[0], stop=k == sum_order[-1])
+                        banks[i, part.start, m] = bank
+                    finished = [(i, part)]
+        for done in finished:
+            store(*done)

import concourse.mybir as mybir

P = 128
PIECE = 512
HEAD = 2
TAIL = 2
BANKS = 8
FLOPS = 2 * 256 * 256 * 2048

F32, BF16, U16 = mybir.dt.float32, mybir.dt.bfloat16, mybir.dt.uint16
RELU = mybir.ActivationFunctionType.Relu
MULT = mybir.AluOpType.mult


def tile_lookup_gate_relu_none_kernel(tc, tab, y, w, offs, out):
    nc = tc.nc
    rows, window_cols = tab.shape
    out_rows, entries = out.shape
    blocks, out_blocks, pieces = rows // P, out_rows // P, entries // PIECE
    offset_cols = PIECE // 16

    with (
        tc.tile_pool(name="held", bufs=1) as held,
        tc.psum_pool(name="psum", bufs=BANKS) as psum,
    ):
        offsets = held.tile([P, entries // 16], U16, name="offsets")
        nc.sync.dma_start(offsets[:], offs)
        windows = [held.tile([P, window_cols], F32, name=f"window{b}") for b in range(blocks)]
        for b in range(blocks):
            nc.sync.dma_start(windows[b][:], tab[b * P : (b + 1) * P, :])
        weights = held.tile([P, blocks, out_rows], BF16, name="weights")

        warm_in = held.tile([P, 8], F32, name="warm_in")
        warm_out = held.tile([P, 8], F32, name="warm_out")
        nc.vector.memset(warm_in[:], 0.0)
        nc.scalar.activation(warm_out[:], warm_in[:], RELU)

        steps = [(b, i) for b in range(blocks) for i in range(HEAD)]
        steps += [(b, i) for i in range(HEAD, pieces) for b in range(blocks)]
        stream = {}
        for b, i in steps:
            stream[b, i] = held.tile([P, PIECE], F32, name=f"stream{b}_{i}")
            nc.sync.dma_start(stream[b, i][:], y[b * P : (b + 1) * P, i * PIECE : (i + 1) * PIECE])
            if (b, i) == steps[0]:
                nc.sync.dma_start(weights[:], w.rearrange("(b p) m -> p b m", p=P))

        gates = [held.tile([P, PIECE], F32, name=f"gate{k}") for k in range(blocks * HEAD)]
        xs = [held.tile([P, PIECE], BF16, name=f"x{k}") for k in range(HEAD + 2)]
        banks = {}

        def parts(i):
            width = PIECE // TAIL if i == pieces - 1 else PIECE
            return [slice(first, first + width) for first in range(0, PIECE, width)]

        def store(i, part):
            for m in range(out_blocks):
                result = held.tile([P, part.stop - part.start], F32, name=f"result{i}_{part.start}_{m}")
                if i >= pieces - 2 and m == 1:
                    nc.scalar.copy(result[:], banks[i, part.start, m][:])
                else:
                    nc.vector.tensor_copy(result[:], banks[i, part.start, m][:])
                nc.sync.dma_start(out[m * P : (m + 1) * P, i * PIECE + part.start : i * PIECE + part.stop], result[:])

        x_of = {}
        finished = []
        for step, (b, i) in enumerate(steps):
            gate = gates[step % len(gates)]
            nc.scalar.activation(gate[:], windows[b][:].indirect(offsets[:, i * offset_cols : (i + 1) * offset_cols]), RELU)
            x_of[b, i] = xs[step if step < HEAD else HEAD + step % 2]
            multiplier = nc.gpsimd if step == blocks * HEAD else nc.vector
            sum_order = (1, 0) if 0 < i < HEAD else (0, 1)
            for part in parts(i):
                multiplier.tensor_tensor(x_of[b, i][:, part], gate[:, part], stream[b, i][:, part], MULT)
                for done in finished:
                    store(*done)
                finished = []
                if b == blocks - 1:
                    for m in range(out_blocks):
                        bank = psum.tile([P, part.stop - part.start], F32, name="bank")
                        for k in sum_order:
                            nc.tensor.matmul(bank[:], weights[:, k, m * P : (m + 1) * P], x_of[k, i][:, part], start=k == sum_order[0], stop=k == sum_order[-1])
                        banks[i, part.start, m] = bank
                    finished = [(i, part)]
        for done in finished:
            store(*done)
